import numpy as np
import ml_dtypes


def mxq(x, axis, fmt="e4m3"):
    dtype, down = {"e4m3": (ml_dtypes.float8_e4m3fn, 7), "e5m2": (ml_dtypes.float8_e5m2, 14)}[fmt]
    v = np.moveaxis(np.asarray(x, np.float32).astype(ml_dtypes.bfloat16).astype(np.float64), axis, -1)
    blocks = v.reshape(v.shape[:-1] + (-1, 32))
    amax = np.abs(blocks).max(-1, keepdims=True)
    byte = np.maximum(np.where(amax > 0, np.frexp(amax)[1] - 1 + 127, 0) - down, 1)
    scale = np.exp2(byte - 127.0)
    codes = (blocks / scale).astype(np.float32).astype(dtype).astype(np.float64)
    return np.moveaxis((codes * scale).reshape(v.shape), -1, axis)


WIDE = False


def mx_kscale(k):
    if not WIDE:
        return np.ones(k)
    levels = np.array([10, -10, 5, -5, 0])
    if k % 512:
        return np.exp2(np.random.permutation(np.resize(levels, k // 32))).repeat(32)
    a = np.empty((k // 512, 16))
    for p in range(k // 512):
        a[p, :8] = np.random.permutation(np.resize(levels, 8))
        for g in range(8):
            far = levels[np.abs(levels - a[p, g]) >= 10]
            a[p, g + 8] = far[np.random.randint(len(far))]
    return np.exp2(a.ravel()).repeat(32)


def f64(x):
    return np.asarray(x).astype(np.float64)


def striped(idx):
    return np.tile(idx.reshape(-1, 16).T, (8, 1)).astype(np.uint16)


def unstriped(offs):
    return offs[:16].T.reshape(-1).astype(np.int64)


def pack_weight(w):
    k, n = w.shape
    w = f64(np.asarray(w, np.float32).astype(ml_dtypes.bfloat16)).reshape(k // 32, 32, n)
    amax = np.abs(w).max(1)
    byte = np.clip(np.where(amax > 0, np.frexp(amax)[1] - 1 + 127 - 7, 1), 1, 254)
    scaled = (w * np.exp2(127.0 - byte)[:, None, :]).reshape(k, n).astype(np.float32)
    words = np.ascontiguousarray(scaled.reshape(k // 512, 128, 4, n).transpose(0, 1, 3, 2)).astype(ml_dtypes.float8_e4m3fn).view(np.uint8)
    return words, np.ascontiguousarray(byte.astype(np.uint8).reshape(k // 512, 16, n))


def unpack_weight(words, scales):
    g, p, n, _ = words.shape
    vals = np.ascontiguousarray(words).view(ml_dtypes.float8_e4m3fn).astype(np.float64) * np.repeat(np.exp2(scales.astype(np.float64) - 127.0), 8, axis=1)[..., None]
    return vals.transpose(0, 1, 3, 2).reshape(g * 512, n)


K, T, S, D, H, Z, W = 512, 2048, 512, 2, 512, 512, 2048
P = 2 ** 7


def setup_inputs():
    n = np.random.standard_normal
    s = mx_kscale(K)[:, None]
    packed_xT = pack_weight(n((K, T)) * s)
    packed_eT = pack_weight(n((K, W)) * s)
    return {
        "x_words": packed_xT[0],
        "x_scales": packed_xT[1],
        "w1": (n((K, H)) / np.sqrt(K) / s).astype(np.float32),
        "e_words": packed_eT[0],
        "e_scales": packed_eT[1],
        "unit": (np.random.uniform(0.6, 1.4, (K, 1)) / np.sqrt(K) / s).astype(np.float32),
        "len_": (np.tile(np.random.uniform(0.4, 1.6, W), (P, 1))).astype(np.float32),
        "offs": striped(np.random.permutation(T)[:S]),
        "nxt": striped(np.random.permutation(S)),
        "road": striped(np.random.permutation(W)[:Z]),
        "con": striped(np.random.permutation(Z)),
    }


def reference(x_words, x_scales, w1, e_words, e_scales, unit, len_, offs, nxt, road, con):
    xq = unpack_weight(x_words, x_scales)[:, unstriped(offs)]
    y = mxq(f64(w1), 0, "e4m3").T @ xq
    yn = y[:, unstriped(nxt)]
    vel = yn - y
    vy = vel * np.abs(y)
    traj = vy.reshape(len(vy), -1, D).sum(axis=2)
    tn = traj / (np.abs(traj) + 0.8)
    hid = f64(unit) * tn
    e_road = unpack_weight(e_words, e_scales)[:, unstriped(road)]
    sc = mxq(hid, 0, "e4m3").T @ e_road
    ds = sc - (f64(len_)[:1][:, unstriped(road)])
    emis = -1.0 * ((ds) ** 2)
    prevm = emis[:, unstriped(con)]
    return np.log(np.exp(emis) + np.exp(0.7 * prevm))

@@ -1,0 +1,255 @@
+from contextlib import ExitStack
+import math
+
+import concourse.mybir as mybir
+
+K, T, S, H, Z, W = 512, 2048, 512, 512, 512, 2048
+V = S // 2
+FLOPS = 2 * K * H * S + 2 * H * V * Z
+
+F32 = mybir.dt.float32
+BF16 = mybir.dt.bfloat16
+I32 = mybir.dt.int32
+U32 = mybir.dt.uint32
+U16 = mybir.dt.uint16
+U8 = mybir.dt.uint8
+FP8X4 = mybir.dt.float8_e4m3fn_x4
+ALU = mybir.AluOpType
+ACT = mybir.ActivationFunctionType
+
+P = 128
+PACK = 4
+HALF = 256
+HC = HALF // 16
+
+
+def tile_picked_ytrajcl_lse_p_kernel(
+    tc, x_words, x_scales, w1, e_words, e_scales, unit, len_, offs, nxt, road, con, out
+):
+    nc = tc.nc
+    with ExitStack() as ctx:
+        sb = ctx.enter_context(tc.tile_pool(name="sb", bufs=1))
+        ps = ctx.enter_context(tc.psum_pool(name="ps", bufs=1))
+
+        def tl(name, shape, dtype):
+            return sb.tile(shape, dtype, name=name, align_bytes=64)
+
+        offs_t = tl("offs_t", [P, S // 16], U16)
+        nxt_t = tl("nxt_t", [P, S // 16], U16)
+        road_t = tl("road_t", [P, Z // 16], U16)
+        con_t = tl("con_t", [P, Z // 16], U16)
+        xs = tl("xs", [P, T], U8)
+        es = tl("es", [P, W], U8)
+        u = tl("u", [P, PACK], F32)
+        w_raw = sb.tile([P, PACK, H], F32, name="w_raw", tag="first", align_bytes=64)
+        xw = sb.tile([P, T], I32, name="xw", tag="second", align_bytes=64)
+
+        nc.vector.memset(xs[:].bitcast(I32), 0)
+        nc.vector.memset(es[:].bitcast(I32), 0)
+
+        def load_scales(queue, dst, src, q):
+            queue.dma_start(out=dst[32 * q : 32 * q + 4, :].bitcast(I32), in_=src[0, 4 * q : 4 * q + 4, :].bitcast(I32))
+
+        def words(src):
+            return src[0].rearrange("p n t -> p (n t)").bitcast(I32)
+
+        nc.sync.dma_start(out=w_raw[:], in_=w1.rearrange("(p j) c -> p j c", j=PACK))
+        nc.sync.dma_start(offs_t[:], offs)
+        nc.sync.dma_start(out=xw[:], in_=words(x_words))
+        nc.sync.dma_start(road_t[:], road)
+        nc.sync.dma_start(nxt_t[:], nxt)
+        nc.sync.dma_start(con_t[:], con)
+        nc.gpsimd.dma_start(out=u[:], in_=unit.rearrange("(p t) o -> p (t o)", t=PACK))
+        for q in range(4):
+            load_scales(nc.scalar if q < 2 else nc.gpsimd, xs, x_scales, q)
+        for q in range(4):
+            load_scales(nc.sync if q < 2 else nc.gpsimd, es, e_scales, q)
+
+        xg_s = tl("xg_s", [P, S], U8)
+        xg_w = tl("xg_w", [P, S], U32)
+
+        nc.vector.tensor_copy(xg_s[:], xs[:].indirect(offs_t[:]))
+        u_safe = tl("u_safe", [P, PACK], F32)
+        u_isq = tl("u_isq", [P, PACK], F32)
+        u_inv = tl("u_inv", [P, PACK], F32)
+        nc.vector.scalar_tensor_tensor(u_safe[:], u[:], 0.0, u[:], ALU.is_equal, ALU.add)
+        nc.scalar.activation(u_isq[:], u_safe[:], ACT.Abs_reciprocal_sqrt)
+        nc.scalar.activation(u_inv[:], u_isq[:], ACT.Square)
+
+        w_bf = sb.tile([P, PACK, P, PACK], BF16, name="w_bf", tag="third", align_bytes=64)
+        w_src = w_raw[:].rearrange("p j (m t) -> p m j t", t=PACK)
+        w_dst = w_bf[:].rearrange("p t m j -> p m j t")
+        nc.vector.tensor_copy(w_dst, w_src)
+        ew = sb.tile([P, W], I32, name="ew", tag="first", align_bytes=64)
+        nc.sync.dma_start(out=ew[:], in_=words(e_words))
+        wq_w = tl("wq_w", [P, H], U32)
+        wq_s = tl("wq_s", [P, H], U8)
+        nc.vector.quantize_mx(out=wq_w[:].bitcast(FP8X4), scales=wq_s[:], in_=w_bf[:].rearrange("p t m j -> p (t m j)"))
+        len_t = sb.tile([P, W], F32, name="len_t", tag="third", align_bytes=64)
+        nc.sync.dma_start(out=len_t[:], in_=len_)
+        for c in range(2):
+            nc.vector.tensor_copy(xg_w[:, c * HALF : (c + 1) * HALF], xw[:].bitcast(U32).indirect(offs_t[:, c * HC : (c + 1) * HC]))
+        eg_s = sb.tile([P, Z], U8, name="eg_s", tag="second", align_bytes=64)
+        nc.vector.tensor_copy(eg_s[:], es[:].indirect(road_t[:]))
+
+
+        def tiles(name, n, shape, dtype):
+            return [tl("%s%d" % (name, i), shape, dtype) for i in range(n)]
+
+        y_ps = [ps.tile([P, S], F32, name="y_ps%d" % t) for t in range(PACK)]
+        uy = tiles("uy", PACK, [P, S], F32)
+        mag = tiles("mag", PACK, [P, S], F32)
+        own = tiles("own", PACK, [P, S], F32)
+        vel = tiles("vel", PACK, [P, S], F32)
+        vy = [sb.tile([P, S], F32, name="vy%d" % t, tag="vy%d" % t, align_bytes=64) for t in range(PACK)]
+        y_first = ps.tile([P, HALF], F32, name="y_first")
+        traj = tl("traj", [P, PACK, V], F32)
+        den = tiles("den", PACK, [P, V], F32)
+        den2 = tiles("den2", PACK, [P, V], F32)
+        rec = tl("rec", [P, PACK, V], F32)
+        hid = tiles("hid", 2, [P, P, PACK], BF16)
+        hq_w = tiles("hq_w", 2, [P, P], U32)
+        hq_s = tiles("hq_s", 2, [P, P], U8)
+        sc_ps = [ps.tile([P, Z], F32, name="sc_ps%d" % h) for h in range(2)]
+        len_g = tl("len_g", [P, Z], F32)
+        ds = tiles("ds", 2, [P, Z], F32)
+        sq = tiles("sq", 2, [P, Z], F32)
+        sq7 = tiles("sq7", 2, [P, Z], F32)
+        dif = tiles("dif", 2, [P, Z], F32)
+        gap = tiles("gap", 2, [P, Z], F32)
+        ex = tl("ex", [P, 2, Z], F32)
+        low = tl("low", [P, 2, Z], F32)
+        res = tiles("res", 2, [P, Z], F32)
+
+        halves = [slice(0, HALF), slice(HALF, S)]
+        whole = slice(0, S)
+
+        def product(t, dst, cols):
+            rows = slice(t * P, (t + 1) * P)
+            nc.tensor.matmul_mx(
+                out=dst, lhsT=wq_w[:, rows].bitcast(FP8X4), lhsT_scale=wq_s[:, rows],
+                rhs=xg_w[:, cols].bitcast(FP8X4), rhs_scale=xg_s[:, cols], start=True, stop=True,
+            )
+
+        def scaled(t, dst, src):
+            nc.scalar.activation(dst, src, ACT.Copy, scale=u[:, t : t + 1])
+
+        product(0, y_first[:], halves[0])
+        product(0, y_ps[0][:, halves[1]], halves[1])
+        scaled(0, uy[0][:, halves[0]], y_first[:])
+        scaled(0, uy[0][:, halves[1]], y_ps[0][:, halves[1]])
+        nc.scalar.activation(mag[0][:, halves[0]], y_first[:], ACT.Abs)
+        nc.scalar.activation(mag[0][:, halves[1]], y_ps[0][:, halves[1]], ACT.Abs)
+        for t in range(1, PACK):
+            product(t, y_ps[t][:], whole)
+            scaled(t, uy[t][:], y_ps[t][:])
+            nc.scalar.activation(mag[t][:], y_ps[t][:], ACT.Abs)
+        scaled(PACK - 1, own[PACK - 1][:], y_ps[PACK - 1][:])
+
+        def copy_own(t, cols):
+            nc.vector.tensor_copy(own[t][:, cols], uy[t][:, cols])
+
+        def step(t, c):
+            cols = halves[c]
+            nc.vector.tensor_tensor(vel[t][:, cols], uy[t][:].indirect(nxt_t[:, c * HC : (c + 1) * HC]), own[t][:, cols], ALU.subtract)
+
+        def weigh(t, cols):
+            nc.vector.tensor_tensor(vy[t][:, cols], vel[t][:, cols], mag[t][:, cols], ALU.mult)
+
+        def pair(t, cols):
+            vs = slice(cols.start // 2, cols.stop // 2)
+            pairs = vy[t][:, cols].rearrange("p (v d) -> p v d", d=2)
+            nc.vector.tensor_tensor(traj[:, t, vs], pairs[:, :, 0], pairs[:, :, 1], ALU.add)
+            nc.scalar.activation(den[t][:, vs], traj[:, t, vs], ACT.Abs, scale=u_inv[:, t : t + 1])
+            nc.scalar.activation(den2[t][:, vs], den[t][:, vs], ACT.Square, bias=0.8)
+            nc.scalar.activation(rec[:, t, vs], den2[t][:, vs], ACT.Abs_reciprocal_sqrt)
+
+        def hidden(h):
+            cols = slice(h * P, (h + 1) * P)
+            nc.vector.tensor_tensor(
+                hid[h][:].rearrange("p (c i) t -> p c t i", i=4),
+                traj[:, :, cols].rearrange("p t (c i) -> p c t i", i=4),
+                rec[:, :, cols].rearrange("p t (c i) -> p c t i", i=4),
+                ALU.mult,
+            )
+
+        def scores(h):
+            nc.vector.quantize_mx(out=hq_w[h][:].bitcast(FP8X4), scales=hq_s[h][:], in_=hid[h][:].rearrange("p v t -> p (v t)"))
+            nc.tensor.matmul_mx(
+                out=sc_ps[h][:], lhsT=hq_w[h][:].bitcast(FP8X4), lhsT_scale=hq_s[h][:],
+                rhs=eg_w[:].bitcast(FP8X4), rhs_scale=eg_s[:], start=True, stop=True,
+            )
+
+        def distances(h):
+            nc.vector.tensor_tensor(ds[h][:], sc_ps[h][:], len_g[:], ALU.subtract)
+
+        def squares(h):
+            nc.scalar.activation(sq7[h][:], ds[h][:], ACT.Square, scale=math.sqrt(0.7))
+            if h == 0:
+                nc.vector.tensor_tensor(sq[h][:], ds[h][:], ds[h][:], ALU.mult)
+            else:
+                nc.scalar.activation(sq[h][:], ds[h][:], ACT.Square)
+
+        def differences(h):
+            for c in range(2):
+                cols = slice(c * HALF, (c + 1) * HALF)
+                nc.vector.tensor_tensor(dif[h][:, cols], sq7[h][:].indirect(con_t[:, c * HC : (c + 1) * HC]), sq[h][:, cols], ALU.subtract)
+            for c in range(2):
+                cols = slice(c * HALF, (c + 1) * HALF)
+                nc.scalar.activation(gap[h][:, cols], dif[h][:, cols], ACT.Abs)
+                nc.scalar.activation(ex[:, h, cols], gap[h][:, cols], ACT.Exp, scale=-1.0)
+
+        def smaller(h):
+            nc.vector.scalar_tensor_tensor(low[:, h, :], dif[h][:], 0.0, sq[h][:], ALU.min, ALU.add)
+
+        def finish(h, cols):
+            lg = gap[1 - h]
+            nc.scalar.activation(lg[:, cols], ex[:, h, cols], ACT.Ln, bias=1.0)
+            nc.vector.tensor_tensor(res[h][:, cols], lg[:, cols], low[:, h, cols], ALU.subtract)
+            nc.sync.dma_start(out=out[h * P : (h + 1) * P, cols], in_=res[h][:, cols])
+
+        last = PACK - 1
+        copy_own(0, halves[0])
+        step(0, 0)
+        copy_own(0, halves[1])
+        step(0, 1)
+        copy_own(1, whole)
+        weigh(0, whole)
+        for t in range(1, last):
+            step(t, 0)
+            pair(t - 1, whole)
+            step(t, 1)
+            if t + 1 < last:
+                copy_own(t + 1, whole)
+            weigh(t, whole)
+            if t == 1:
+                nc.scalar.activation(len_g[:], len_t[:].indirect(road_t[:]), ACT.Copy)
+        step(last, 0)
+        pair(last - 1, whole)
+        eg_w = sb.tile([P, Z], U32, name="eg_w", tag="vy%d" % (last - 1), align_bytes=64)
+
+        def fetch_roads(c):
+            nc.vector.tensor_copy(eg_w[:, halves[c]], ew[:].bitcast(U32).indirect(road_t[:, c * HC : (c + 1) * HC]))
+
+        weigh(last, halves[0])
+        step(last, 1)
+        pair(last, halves[0])
+        weigh(last, halves[1])
+        fetch_roads(0)
+        pair(last, halves[1])
+        fetch_roads(1)
+        hidden(0)
+        scores(0)
+        hidden(1)
+        scores(1)
+        distances(0)
+        distances(1)
+        squares(0)
+        squares(1)
+        differences(0)
+        differences(1)
+        smaller(0)
+        smaller(1)
+        finish(0, slice(0, Z))
+        finish(1, slice(0, HALF))
+        finish(1, slice(HALF, Z))

@@ -21,6 +21,7 @@ P = 128
 PACK = 4
 HALF = 256
 HC = HALF // 16
+M_VEC = 80
 
 
 def tile_picked_ytrajcl_lse_p_kernel(
@@ -38,13 +39,12 @@ def tile_picked_ytrajcl_lse_p_kernel(
         nxt_t = tl("nxt_t", [P, S // 16], U16)
         road_t = tl("road_t", [P, Z // 16], U16)
         con_t = tl("con_t", [P, Z // 16], U16)
-        xs = tl("xs", [P, T], U8)
+        xs = sb.tile([P, T], U8, name="xs", tag="fourth", align_bytes=64)
         es = tl("es", [P, W], U8)
         u = tl("u", [P, PACK], F32)
         w_raw = sb.tile([P, PACK, H], F32, name="w_raw", tag="first", align_bytes=64)
         xw = sb.tile([P, T], I32, name="xw", tag="second", align_bytes=64)
 
-        nc.vector.memset(xs[:].bitcast(I32), 0)
         nc.vector.memset(es[:].bitcast(I32), 0)
 
         def load_scales(queue, dst, src, q):
@@ -53,22 +53,26 @@ def tile_picked_ytrajcl_lse_p_kernel(
         def words(src):
             return src[0].rearrange("p n t -> p (n t)").bitcast(I32)
 
-        nc.sync.dma_start(out=w_raw[:], in_=w1.rearrange("(p j) c -> p j c", j=PACK))
+        nc.sync.dma_start(out=u[:], in_=unit.rearrange("(p t) o -> p (t o)", t=PACK))
         nc.sync.dma_start(offs_t[:], offs)
         nc.sync.dma_start(out=xw[:], in_=words(x_words))
+        nc.sync.dma_start(out=w_raw[:], in_=w1.rearrange("(p j) c -> p j c", j=PACK))
+        for q in range(4):
+            rows = x_scales[0, 4 * q : 4 * q + 4, :].bitcast(I32)
+            nc.scalar.dma_start(out=xs[32 * q : 32 * q + 32, :].bitcast(I32), in_=rows.unsqueeze(0).to_broadcast([8, 4, T // 4]))
         nc.sync.dma_start(road_t[:], road)
         nc.sync.dma_start(nxt_t[:], nxt)
         nc.sync.dma_start(con_t[:], con)
-        nc.gpsimd.dma_start(out=u[:], in_=unit.rearrange("(p t) o -> p (t o)", t=PACK))
-        for q in range(4):
-            load_scales(nc.scalar if q < 2 else nc.gpsimd, xs, x_scales, q)
         for q in range(4):
             load_scales(nc.sync if q < 2 else nc.gpsimd, es, e_scales, q)
 
-        xg_s = tl("xg_s", [P, S], U8)
         xg_w = tl("xg_w", [P, S], U32)
 
+        nc.vector.tensor_copy(xg_w[:], xw[:].bitcast(U32).indirect(offs_t[:]))
+        xg_s = sb.tile([P, S], U8, name="xg_s", tag="second", align_bytes=64)
         nc.vector.tensor_copy(xg_s[:], xs[:].indirect(offs_t[:]))
+        len_t = sb.tile([P, W], F32, name="len_t", tag="fourth", align_bytes=64)
+        nc.sync.dma_start(out=len_t[:], in_=len_)
         u_safe = tl("u_safe", [P, PACK], F32)
         u_isq = tl("u_isq", [P, PACK], F32)
         u_inv = tl("u_inv", [P, PACK], F32)
@@ -79,26 +83,25 @@ def tile_picked_ytrajcl_lse_p_kernel(
         w_bf = sb.tile([P, PACK, P, PACK], BF16, name="w_bf", tag="third", align_bytes=64)
         w_src = w_raw[:].rearrange("p j (m t) -> p m j t", t=PACK)
         w_dst = w_bf[:].rearrange("p t m j -> p m j t")
-        nc.vector.tensor_copy(w_dst, w_src)
+        nc.vector.tensor_copy(w_dst[:, :M_VEC], w_src[:, :M_VEC])
+        nc.scalar.copy(w_dst[:, M_VEC:], w_src[:, M_VEC:])
         ew = sb.tile([P, W], I32, name="ew", tag="first", align_bytes=64)
         nc.sync.dma_start(out=ew[:], in_=words(e_words))
         wq_w = tl("wq_w", [P, H], U32)
         wq_s = tl("wq_s", [P, H], U8)
-        nc.vector.quantize_mx(out=wq_w[:].bitcast(FP8X4), scales=wq_s[:], in_=w_bf[:].rearrange("p t m j -> p (t m j)"))
-        len_t = sb.tile([P, W], F32, name="len_t", tag="third", align_bytes=64)
-        nc.sync.dma_start(out=len_t[:], in_=len_)
-        for c in range(2):
-            nc.vector.tensor_copy(xg_w[:, c * HALF : (c + 1) * HALF], xw[:].bitcast(U32).indirect(offs_t[:, c * HC : (c + 1) * HC]))
-        eg_s = sb.tile([P, Z], U8, name="eg_s", tag="second", align_bytes=64)
+        w_flat = w_bf[:].rearrange("p t m j -> p (t m j)")
+        nc.vector.quantize_mx(out=wq_w[:, :P].bitcast(FP8X4), scales=wq_s[:, :P], in_=w_flat[:, : P * PACK])
+        nc.vector.quantize_mx(out=wq_w[:, P:].bitcast(FP8X4), scales=wq_s[:, P:], in_=w_flat[:, P * PACK :])
+        eg_s = sb.tile([P, Z], U8, name="eg_s", tag="third", align_bytes=64)
         nc.vector.tensor_copy(eg_s[:], es[:].indirect(road_t[:]))
-
 
         def tiles(name, n, shape, dtype):
             return [tl("%s%d" % (name, i), shape, dtype) for i in range(n)]
 
         y_ps = [ps.tile([P, S], F32, name="y_ps%d" % t) for t in range(PACK)]
-        uy = tiles("uy", PACK, [P, S], F32)
-        mag = tiles("mag", PACK, [P, S], F32)
+        win = [tl("win%d" % t, [P, 2 * S if t in (1, 2) else S], F32) for t in range(PACK)]
+        uy = [win[t][:, :S] for t in range(PACK)]
+        mag = [win[t][:, S:] if t in (1, 2) else tl("mag%d" % t, [P, S], F32)[:] for t in range(PACK)]
         own = tiles("own", PACK, [P, S], F32)
         vel = tiles("vel", PACK, [P, S], F32)
         vy = [sb.tile([P, S], F32, name="vy%d" % t, tag="vy%d" % t, align_bytes=64) for t in range(PACK)]
@@ -112,9 +115,10 @@ def tile_picked_ytrajcl_lse_p_kernel(
         hq_s = tiles("hq_s", 2, [P, P], U8)
         sc_ps = [ps.tile([P, Z], F32, name="sc_ps%d" % h) for h in range(2)]
         len_g = tl("len_g", [P, Z], F32)
-        ds = tiles("ds", 2, [P, Z], F32)
+        dwin = tiles("dwin", 2, [P, 2 * Z], F32)
+        ds = [dwin[h][:, Z:] for h in range(2)]
         sq = tiles("sq", 2, [P, Z], F32)
-        sq7 = tiles("sq7", 2, [P, Z], F32)
+        sq7 = [dwin[h][:, :Z] for h in range(2)]
         dif = tiles("dif", 2, [P, Z], F32)
         gap = tiles("gap", 2, [P, Z], F32)
         ex = tl("ex", [P, 2, Z], F32)
@@ -142,16 +146,19 @@ def tile_picked_ytrajcl_lse_p_kernel(
         nc.scalar.activation(mag[0][:, halves[1]], y_ps[0][:, halves[1]], ACT.Abs)
         for t in range(1, PACK):
             product(t, y_ps[t][:], whole)
-            scaled(t, uy[t][:], y_ps[t][:])
-            nc.scalar.activation(mag[t][:], y_ps[t][:], ACT.Abs)
-        scaled(PACK - 1, own[PACK - 1][:], y_ps[PACK - 1][:])
+            scaled(t, uy[t], y_ps[t][:])
+            if t > 1:
+                nc.sync.dma_start(out=own[t][:], in_=uy[t])
+            nc.scalar.activation(mag[t], y_ps[t][:], ACT.Abs)
 
         def copy_own(t, cols):
             nc.vector.tensor_copy(own[t][:, cols], uy[t][:, cols])
 
-        def step(t, c):
-            cols = halves[c]
-            nc.vector.tensor_tensor(vel[t][:, cols], uy[t][:].indirect(nxt_t[:, c * HC : (c + 1) * HC]), own[t][:, cols], ALU.subtract)
+        def entries(lst, cols):
+            return lst[:, cols.start // 16 : cols.stop // 16]
+
+        def step(t, cols):
+            nc.vector.tensor_tensor(vel[t][:, cols], win[t][:].indirect(entries(nxt_t, cols)), own[t][:, cols], ALU.subtract)
 
         def weigh(t, cols):
             nc.vector.tensor_tensor(vy[t][:, cols], vel[t][:, cols], mag[t][:, cols], ALU.mult)
@@ -180,51 +187,47 @@ def tile_picked_ytrajcl_lse_p_kernel(
                 rhs=eg_w[:].bitcast(FP8X4), rhs_scale=eg_s[:], start=True, stop=True,
             )
 
-        def distances(h):
-            nc.vector.tensor_tensor(ds[h][:], sc_ps[h][:], len_g[:], ALU.subtract)
+        def distances(h, cols):
+            nc.vector.tensor_tensor(ds[h][:, cols], sc_ps[h][:, cols], len_g[:, cols], ALU.subtract)
 
-        def squares(h):
-            nc.scalar.activation(sq7[h][:], ds[h][:], ACT.Square, scale=math.sqrt(0.7))
-            if h == 0:
-                nc.vector.tensor_tensor(sq[h][:], ds[h][:], ds[h][:], ALU.mult)
-            else:
-                nc.scalar.activation(sq[h][:], ds[h][:], ACT.Square)
+        def window_squares(h, cols):
+            nc.scalar.activation(sq7[h][:, cols], ds[h][:, cols], ACT.Square, scale=math.sqrt(0.7))
 
-        def differences(h):
-            for c in range(2):
-                cols = slice(c * HALF, (c + 1) * HALF)
-                nc.vector.tensor_tensor(dif[h][:, cols], sq7[h][:].indirect(con_t[:, c * HC : (c + 1) * HC]), sq[h][:, cols], ALU.subtract)
-            for c in range(2):
-                cols = slice(c * HALF, (c + 1) * HALF)
-                nc.scalar.activation(gap[h][:, cols], dif[h][:, cols], ACT.Abs)
-                nc.scalar.activation(ex[:, h, cols], gap[h][:, cols], ACT.Exp, scale=-1.0)
+        def squares(h, cols):
+            nc.scalar.activation(sq[h][:, cols], ds[h][:, cols], ACT.Square)
+
+        def difference(h, cols):
+            nc.vector.tensor_tensor(dif[h][:, cols], dwin[h][:].indirect(entries(con_t, cols)), sq[h][:, cols], ALU.subtract)
+
+        def gaps(h, cols):
+            nc.scalar.activation(gap[h][:, cols], dif[h][:, cols], ACT.Abs)
+
+        def decay(h, cols):
+            nc.scalar.activation(ex[:, h, cols], gap[h][:, cols], ACT.Exp, scale=-1.0)
 
         def smaller(h):
             nc.vector.scalar_tensor_tensor(low[:, h, :], dif[h][:], 0.0, sq[h][:], ALU.min, ALU.add)
 
         def finish(h, cols):
-            lg = gap[1 - h]
+            lg = gap[1] if h == 0 else ex[:, 0, :]
             nc.scalar.activation(lg[:, cols], ex[:, h, cols], ACT.Ln, bias=1.0)
             nc.vector.tensor_tensor(res[h][:, cols], lg[:, cols], low[:, h, cols], ALU.subtract)
             nc.sync.dma_start(out=out[h * P : (h + 1) * P, cols], in_=res[h][:, cols])
 
         last = PACK - 1
         copy_own(0, halves[0])
-        step(0, 0)
+        step(0, halves[0])
         copy_own(0, halves[1])
-        step(0, 1)
+        step(0, halves[1])
         copy_own(1, whole)
         weigh(0, whole)
         for t in range(1, last):
-            step(t, 0)
+            step(t, whole)
             pair(t - 1, whole)
-            step(t, 1)
-            if t + 1 < last:
-                copy_own(t + 1, whole)
             weigh(t, whole)
             if t == 1:
                 nc.scalar.activation(len_g[:], len_t[:].indirect(road_t[:]), ACT.Copy)
-        step(last, 0)
+        step(last, halves[0])
         pair(last - 1, whole)
         eg_w = sb.tile([P, Z], U32, name="eg_w", tag="vy%d" % (last - 1), align_bytes=64)
 
@@ -232,22 +235,38 @@ def tile_picked_ytrajcl_lse_p_kernel(
             nc.vector.tensor_copy(eg_w[:, halves[c]], ew[:].bitcast(U32).indirect(road_t[:, c * HC : (c + 1) * HC]))
 
         weigh(last, halves[0])
-        step(last, 1)
+        step(last, halves[1])
         pair(last, halves[0])
         weigh(last, halves[1])
         fetch_roads(0)
         pair(last, halves[1])
         fetch_roads(1)
+        warm = tl("warm", [P, 1], F32)
+        nc.scalar.activation(warm[:], rec[:, last, V - 1 : V], ACT.Exp)
         hidden(0)
         scores(0)
         hidden(1)
         scores(1)
-        distances(0)
-        distances(1)
-        squares(0)
-        squares(1)
-        differences(0)
-        differences(1)
+        first, second = halves
+        distances(0, first)
+        distances(0, second)
+        window_squares(0, first)
+        window_squares(0, second)
+        nc.vector.tensor_tensor(sq[0][:, first], ds[0][:, first], ds[0][:, first], ALU.mult)
+        squares(0, second)
+        distances(1, whole)
+        difference(0, whole)
+        window_squares(1, whole)
+        squares(1, first)
+        squares(1, second)
+        difference(1, first)
+        difference(1, second)
+        gaps(0, whole)
+        gaps(1, first)
+        decay(0, whole)
+        nc.vector.scalar_tensor_tensor(gap[1][:, second], dif[1][:, second], -1.0, dif[1][:, second], ALU.mult, ALU.max)
+        decay(1, first)
+        decay(1, second)
         smaller(0)
         smaller(1)
         finish(0, slice(0, Z))

@@ -21,7 +21,6 @@ P = 128
 PACK = 4
 HALF = 256
 HC = HALF // 16
-M_VEC = 80
 
 
 def tile_picked_ytrajcl_lse_p_kernel(
@@ -53,18 +52,18 @@ def tile_picked_ytrajcl_lse_p_kernel(
         def words(src):
             return src[0].rearrange("p n t -> p (n t)").bitcast(I32)
 
-        nc.sync.dma_start(out=u[:], in_=unit.rearrange("(p t) o -> p (t o)", t=PACK))
-        nc.sync.dma_start(offs_t[:], offs)
         nc.sync.dma_start(out=xw[:], in_=words(x_words))
-        nc.sync.dma_start(out=w_raw[:], in_=w1.rearrange("(p j) c -> p j c", j=PACK))
+        nc.scalar.dma_start(out=u[:], in_=unit.rearrange("(p t) o -> p (t o)", t=PACK))
+        nc.sync.dma_start(offs_t[:], offs)
         for q in range(4):
             rows = x_scales[0, 4 * q : 4 * q + 4, :].bitcast(I32)
-            nc.scalar.dma_start(out=xs[32 * q : 32 * q + 32, :].bitcast(I32), in_=rows.unsqueeze(0).to_broadcast([8, 4, T // 4]))
+            nc.sync.dma_start(out=xs[32 * q : 32 * q + 32, :].bitcast(I32), in_=rows.unsqueeze(0).to_broadcast([8, 4, T // 4]))
+        nc.sync.dma_start(out=w_raw[:], in_=w1.rearrange("(p j) c -> p j c", j=PACK))
         nc.sync.dma_start(road_t[:], road)
         nc.sync.dma_start(nxt_t[:], nxt)
         nc.sync.dma_start(con_t[:], con)
         for q in range(4):
-            load_scales(nc.sync if q < 2 else nc.gpsimd, es, e_scales, q)
+            load_scales(nc.sync, es, e_scales, q)
 
         xg_w = tl("xg_w", [P, S], U32)
 
@@ -80,20 +79,27 @@ def tile_picked_ytrajcl_lse_p_kernel(
         nc.scalar.activation(u_isq[:], u_safe[:], ACT.Abs_reciprocal_sqrt)
         nc.scalar.activation(u_inv[:], u_isq[:], ACT.Square)
 
-        w_bf = sb.tile([P, PACK, P, PACK], BF16, name="w_bf", tag="third", align_bytes=64)
-        w_src = w_raw[:].rearrange("p j (m t) -> p m j t", t=PACK)
-        w_dst = w_bf[:].rearrange("p t m j -> p m j t")
-        nc.vector.tensor_copy(w_dst[:, :M_VEC], w_src[:, :M_VEC])
-        nc.scalar.copy(w_dst[:, M_VEC:], w_src[:, M_VEC:])
-        ew = sb.tile([P, W], I32, name="ew", tag="first", align_bytes=64)
-        nc.sync.dma_start(out=ew[:], in_=words(e_words))
+        w_src = w_raw[:].rearrange("p j (m t) -> p t m j", t=PACK)
+        w_bf = [sb.tile([P, P, PACK], BF16, name="w_bf%d" % t, tag="w_bf%d" % t, align_bytes=64) for t in range(PACK)]
         wq_w = tl("wq_w", [P, H], U32)
         wq_s = tl("wq_s", [P, H], U8)
-        w_flat = w_bf[:].rearrange("p t m j -> p (t m j)")
-        nc.vector.quantize_mx(out=wq_w[:, :P].bitcast(FP8X4), scales=wq_s[:, :P], in_=w_flat[:, : P * PACK])
-        nc.vector.quantize_mx(out=wq_w[:, P:].bitcast(FP8X4), scales=wq_s[:, P:], in_=w_flat[:, P * PACK :])
-        eg_s = sb.tile([P, Z], U8, name="eg_s", tag="third", align_bytes=64)
+
+        def quantise_weights(t):
+            cols = slice(t * P, (t + 1) * P)
+            nc.vector.quantize_mx(out=wq_w[:, cols].bitcast(FP8X4), scales=wq_s[:, cols], in_=w_bf[t][:].rearrange("p m j -> p (m j)"))
+
+        nc.vector.tensor_copy(w_bf[0][:], w_src[:, 0])
+        nc.scalar.copy(w_bf[1][:], w_src[:, 1])
+        quantise_weights(0)
+        nc.vector.tensor_copy(w_bf[2][:], w_src[:, 2])
+        nc.scalar.copy(w_bf[3][:], w_src[:, 3])
+        ew = sb.tile([P, W], I32, name="ew", tag="first", align_bytes=64)
+        nc.sync.dma_start(out=ew[:], in_=words(e_words))
+        quantise_weights(1)
+        quantise_weights(2)
+        eg_s = sb.tile([P, Z], U8, name="eg_s", tag="w_bf2", align_bytes=64)
         nc.vector.tensor_copy(eg_s[:], es[:].indirect(road_t[:]))
+        quantise_weights(3)
 
         def tiles(name, n, shape, dtype):
             return [tl("%s%d" % (name, i), shape, dtype) for i in range(n)]
@@ -115,14 +121,13 @@ def tile_picked_ytrajcl_lse_p_kernel(
         hq_s = tiles("hq_s", 2, [P, P], U8)
         sc_ps = [ps.tile([P, Z], F32, name="sc_ps%d" % h) for h in range(2)]
         len_g = tl("len_g", [P, Z], F32)
-        dwin = tiles("dwin", 2, [P, 2 * Z], F32)
+        dwin = [sb.tile([P, 2 * Z], F32, name="dwin%d" % h, tag="dwin%d" % h, align_bytes=64) for h in range(2)]
         ds = [dwin[h][:, Z:] for h in range(2)]
         sq = tiles("sq", 2, [P, Z], F32)
         sq7 = [dwin[h][:, :Z] for h in range(2)]
         dif = tiles("dif", 2, [P, Z], F32)
         gap = tiles("gap", 2, [P, Z], F32)
         ex = tl("ex", [P, 2, Z], F32)
-        low = tl("low", [P, 2, Z], F32)
         res = tiles("res", 2, [P, Z], F32)
 
         halves = [slice(0, HALF), slice(HALF, S)]
@@ -240,10 +245,10 @@ def tile_picked_ytrajcl_lse_p_kernel(
         weigh(last, halves[1])
         fetch_roads(0)
         pair(last, halves[1])
-        fetch_roads(1)
         warm = tl("warm", [P, 1], F32)
         nc.scalar.activation(warm[:], rec[:, last, V - 1 : V], ACT.Exp)
         hidden(0)
+        fetch_roads(1)
         scores(0)
         hidden(1)
         scores(1)
@@ -261,6 +266,7 @@ def tile_picked_ytrajcl_lse_p_kernel(
         squares(1, second)
         difference(1, first)
         difference(1, second)
+        low = sb.tile([P, 2, Z], F32, name="low", tag="dwin1", align_bytes=64)
         gaps(0, whole)
         gaps(1, first)
         decay(0, whole)
@@ -270,5 +276,5 @@ def tile_picked_ytrajcl_lse_p_kernel(
         smaller(0)
         smaller(1)
         finish(0, slice(0, Z))
-        finish(1, slice(0, HALF))
-        finish(1, slice(HALF, Z))
+        finish(1, slice(0, 3 * P))
+        finish(1, slice(3 * P, Z))

@@ -39,7 +39,7 @@ def tile_picked_ytrajcl_lse_p_kernel(
         road_t = tl("road_t", [P, Z // 16], U16)
         con_t = tl("con_t", [P, Z // 16], U16)
         xs = sb.tile([P, T], U8, name="xs", tag="fourth", align_bytes=64)
-        es = tl("es", [P, W], U8)
+        es = sb.tile([P, W], U8, name="es", tag="fifth", align_bytes=64)
         u = tl("u", [P, PACK], F32)
         w_raw = sb.tile([P, PACK, H], F32, name="w_raw", tag="first", align_bytes=64)
         xw = sb.tile([P, T], I32, name="xw", tag="second", align_bytes=64)
@@ -52,13 +52,13 @@ def tile_picked_ytrajcl_lse_p_kernel(
         def words(src):
             return src[0].rearrange("p n t -> p (n t)").bitcast(I32)
 
-        nc.sync.dma_start(out=xw[:], in_=words(x_words))
-        nc.scalar.dma_start(out=u[:], in_=unit.rearrange("(p t) o -> p (t o)", t=PACK))
+        nc.sync.dma_start(out=u[:], in_=unit.rearrange("(p t) o -> p (t o)", t=PACK))
+        nc.sync.dma_start(out=w_raw[:], in_=w1.rearrange("(p j) c -> p j c", j=PACK))
         nc.sync.dma_start(offs_t[:], offs)
         for q in range(4):
             rows = x_scales[0, 4 * q : 4 * q + 4, :].bitcast(I32)
             nc.sync.dma_start(out=xs[32 * q : 32 * q + 32, :].bitcast(I32), in_=rows.unsqueeze(0).to_broadcast([8, 4, T // 4]))
-        nc.sync.dma_start(out=w_raw[:], in_=w1.rearrange("(p j) c -> p j c", j=PACK))
+        nc.sync.dma_start(out=xw[:], in_=words(x_words))
         nc.sync.dma_start(road_t[:], road)
         nc.sync.dma_start(nxt_t[:], nxt)
         nc.sync.dma_start(con_t[:], con)
@@ -67,11 +67,6 @@ def tile_picked_ytrajcl_lse_p_kernel(
 
         xg_w = tl("xg_w", [P, S], U32)
 
-        nc.vector.tensor_copy(xg_w[:], xw[:].bitcast(U32).indirect(offs_t[:]))
-        xg_s = sb.tile([P, S], U8, name="xg_s", tag="second", align_bytes=64)
-        nc.vector.tensor_copy(xg_s[:], xs[:].indirect(offs_t[:]))
-        len_t = sb.tile([P, W], F32, name="len_t", tag="fourth", align_bytes=64)
-        nc.sync.dma_start(out=len_t[:], in_=len_)
         u_safe = tl("u_safe", [P, PACK], F32)
         u_isq = tl("u_isq", [P, PACK], F32)
         u_inv = tl("u_inv", [P, PACK], F32)
@@ -80,26 +75,28 @@ def tile_picked_ytrajcl_lse_p_kernel(
         nc.scalar.activation(u_inv[:], u_isq[:], ACT.Square)
 
         w_src = w_raw[:].rearrange("p j (m t) -> p t m j", t=PACK)
-        w_bf = [sb.tile([P, P, PACK], BF16, name="w_bf%d" % t, tag="w_bf%d" % t, align_bytes=64) for t in range(PACK)]
-        wq_w = tl("wq_w", [P, H], U32)
+        w_bf0 = tl("w_bf0", [P, P, PACK], BF16)
+        w_bf = sb.tile([P, PACK - 1, P, PACK], BF16, name="w_bf", tag="third", align_bytes=64)
+        wq_w0 = tl("wq_w0", [P, P], U32)
         wq_s = tl("wq_s", [P, H], U8)
+        xg_s = tl("xg_s", [P, S], U8)
 
-        def quantise_weights(t):
-            cols = slice(t * P, (t + 1) * P)
-            nc.vector.quantize_mx(out=wq_w[:, cols].bitcast(FP8X4), scales=wq_s[:, cols], in_=w_bf[t][:].rearrange("p m j -> p (m j)"))
-
-        nc.vector.tensor_copy(w_bf[0][:], w_src[:, 0])
-        nc.scalar.copy(w_bf[1][:], w_src[:, 1])
-        quantise_weights(0)
-        nc.vector.tensor_copy(w_bf[2][:], w_src[:, 2])
-        nc.scalar.copy(w_bf[3][:], w_src[:, 3])
+        nc.vector.tensor_copy(w_bf0[:], w_src[:, 0])
+        nc.scalar.copy(w_bf[:, 0], w_src[:, 1])
+        nc.vector.tensor_copy(xg_s[:], xs[:].indirect(offs_t[:]))
+        len_t = sb.tile([P, W], F32, name="len_t", tag="fourth", align_bytes=64)
+        nc.sync.dma_start(out=len_t[:], in_=len_)
+        nc.vector.quantize_mx(out=wq_w0[:].bitcast(FP8X4), scales=wq_s[:, :P], in_=w_bf0[:].rearrange("p m j -> p (m j)"))
+        nc.vector.tensor_copy(w_bf[:, 1], w_src[:, 2])
+        nc.scalar.copy(w_bf[:, 2], w_src[:, 3])
         ew = sb.tile([P, W], I32, name="ew", tag="first", align_bytes=64)
         nc.sync.dma_start(out=ew[:], in_=words(e_words))
-        quantise_weights(1)
-        quantise_weights(2)
-        eg_s = sb.tile([P, Z], U8, name="eg_s", tag="w_bf2", align_bytes=64)
+        for c in range(2):
+            nc.vector.tensor_copy(xg_w[:, c * HALF : (c + 1) * HALF], xw[:].bitcast(U32).indirect(offs_t[:, c * HC : (c + 1) * HC]))
+        wq_w = sb.tile([P, H - P], U32, name="wq_w", tag="second", align_bytes=64)
+        nc.vector.quantize_mx(out=wq_w[:].bitcast(FP8X4), scales=wq_s[:, P:], in_=w_bf[:].rearrange("p t m j -> p (t m j)"))
+        eg_s = sb.tile([P, Z], U8, name="eg_s", tag="third", align_bytes=64)
         nc.vector.tensor_copy(eg_s[:], es[:].indirect(road_t[:]))
-        quantise_weights(3)
 
         def tiles(name, n, shape, dtype):
             return [tl("%s%d" % (name, i), shape, dtype) for i in range(n)]
@@ -108,19 +105,18 @@ def tile_picked_ytrajcl_lse_p_kernel(
         win = [tl("win%d" % t, [P, 2 * S if t in (1, 2) else S], F32) for t in range(PACK)]
         uy = [win[t][:, :S] for t in range(PACK)]
         mag = [win[t][:, S:] if t in (1, 2) else tl("mag%d" % t, [P, S], F32)[:] for t in range(PACK)]
-        own = tiles("own", PACK, [P, S], F32)
+        own_early = sb.tile([P, 2, S], F32, name="own_early", tag="fifth", align_bytes=64)
+        own = [own_early[:, t, :] if t < 2 else tl("own%d" % t, [P, S], F32)[:] for t in range(PACK)]
         vel = tiles("vel", PACK, [P, S], F32)
         vy = [sb.tile([P, S], F32, name="vy%d" % t, tag="vy%d" % t, align_bytes=64) for t in range(PACK)]
-        y_first = ps.tile([P, HALF], F32, name="y_first")
+        y_first = ps.tile([P, HALF], F32, name="y_first", tag="reused")
         traj = tl("traj", [P, PACK, V], F32)
         den = tiles("den", PACK, [P, V], F32)
-        den2 = tiles("den2", PACK, [P, V], F32)
+        den2 = [sb.tile([P, V], F32, name="den2_%d" % t, tag="den2_%d" % t, align_bytes=64) for t in range(PACK)]
         rec = tl("rec", [P, PACK, V], F32)
         hid = tiles("hid", 2, [P, P, PACK], BF16)
         hq_w = tiles("hq_w", 2, [P, P], U32)
         hq_s = tiles("hq_s", 2, [P, P], U8)
-        sc_ps = [ps.tile([P, Z], F32, name="sc_ps%d" % h) for h in range(2)]
-        len_g = tl("len_g", [P, Z], F32)
         dwin = [sb.tile([P, 2 * Z], F32, name="dwin%d" % h, tag="dwin%d" % h, align_bytes=64) for h in range(2)]
         ds = [dwin[h][:, Z:] for h in range(2)]
         sq = tiles("sq", 2, [P, Z], F32)
@@ -135,8 +131,9 @@ def tile_picked_ytrajcl_lse_p_kernel(
 
         def product(t, dst, cols):
             rows = slice(t * P, (t + 1) * P)
+            codes = wq_w0[:] if t == 0 else wq_w[:, (t - 1) * P : t * P]
             nc.tensor.matmul_mx(
-                out=dst, lhsT=wq_w[:, rows].bitcast(FP8X4), lhsT_scale=wq_s[:, rows],
+                out=dst, lhsT=codes.bitcast(FP8X4), lhsT_scale=wq_s[:, rows],
                 rhs=xg_w[:, cols].bitcast(FP8X4), rhs_scale=xg_s[:, cols], start=True, stop=True,
             )
 
@@ -153,7 +150,7 @@ def tile_picked_ytrajcl_lse_p_kernel(
             product(t, y_ps[t][:], whole)
             scaled(t, uy[t], y_ps[t][:])
             if t > 1:
-                nc.sync.dma_start(out=own[t][:], in_=uy[t])
+                nc.sync.dma_start(out=own[t], in_=uy[t])
             nc.scalar.activation(mag[t], y_ps[t][:], ACT.Abs)
 
         def copy_own(t, cols):
@@ -185,15 +182,20 @@ def tile_picked_ytrajcl_lse_p_kernel(
                 ALU.mult,
             )
 
-        def scores(h):
+        def quantise_hidden(h):
             nc.vector.quantize_mx(out=hq_w[h][:].bitcast(FP8X4), scales=hq_s[h][:], in_=hid[h][:].rearrange("p v t -> p (v t)"))
-            nc.tensor.matmul_mx(
-                out=sc_ps[h][:], lhsT=hq_w[h][:].bitcast(FP8X4), lhsT_scale=hq_s[h][:],
-                rhs=eg_w[:].bitcast(FP8X4), rhs_scale=eg_s[:], start=True, stop=True,
-            )
 
-        def distances(h, cols):
-            nc.vector.tensor_tensor(ds[h][:, cols], sc_ps[h][:, cols], len_g[:, cols], ALU.subtract)
+        def scores(h, c):
+            bank = ps.tile([P, HALF], F32, name="sc%d%d" % (h, c), tag="reused" if (h, c) == (1, 1) else "sc%d%d" % (h, c))
+            nc.tensor.matmul_mx(
+                out=bank[:], lhsT=hq_w[h][:].bitcast(FP8X4), lhsT_scale=hq_s[h][:],
+                rhs=eg_w[:, halves[c]].bitcast(FP8X4), rhs_scale=eg_s[:, halves[c]], start=True, stop=True,
+            )
+            return bank
+
+        def distances(h, c, bank):
+            cols = halves[c]
+            nc.vector.tensor_tensor(ds[h][:, cols], bank[:], len_g[:, cols], ALU.subtract)
 
         def window_squares(h, cols):
             nc.scalar.activation(sq7[h][:, cols], ds[h][:, cols], ACT.Square, scale=math.sqrt(0.7))
@@ -221,8 +223,8 @@ def tile_picked_ytrajcl_lse_p_kernel(
 
         last = PACK - 1
         copy_own(0, halves[0])
-        step(0, halves[0])
         copy_own(0, halves[1])
+        step(0, halves[0])
         step(0, halves[1])
         copy_own(1, whole)
         weigh(0, whole)
@@ -231,6 +233,7 @@ def tile_picked_ytrajcl_lse_p_kernel(
             pair(t - 1, whole)
             weigh(t, whole)
             if t == 1:
+                len_g = sb.tile([P, Z], F32, name="len_g", tag="den2_0", align_bytes=64)
                 nc.scalar.activation(len_g[:], len_t[:].indirect(road_t[:]), ACT.Copy)
         step(last, halves[0])
         pair(last - 1, whole)
@@ -247,21 +250,27 @@ def tile_picked_ytrajcl_lse_p_kernel(
         pair(last, halves[1])
         warm = tl("warm", [P, 1], F32)
         nc.scalar.activation(warm[:], rec[:, last, V - 1 : V], ACT.Exp)
-        hidden(0)
-        fetch_roads(1)
-        scores(0)
-        hidden(1)
-        scores(1)
         first, second = halves
-        distances(0, first)
-        distances(0, second)
+        hidden(0)
+        quantise_hidden(0)
+        bank00 = scores(0, 0)
+        fetch_roads(1)
+        bank01 = scores(0, 1)
+        hidden(1)
+        distances(0, 0, bank00)
+        quantise_hidden(1)
+        bank10 = scores(1, 0)
+        bank11 = scores(1, 1)
+        distances(0, 1, bank01)
         window_squares(0, first)
         window_squares(0, second)
         nc.vector.tensor_tensor(sq[0][:, first], ds[0][:, first], ds[0][:, first], ALU.mult)
         squares(0, second)
-        distances(1, whole)
+        distances(1, 0, bank10)
+        distances(1, 1, bank11)
         difference(0, whole)
-        window_squares(1, whole)
+        window_squares(1, first)
+        window_squares(1, second)
         squares(1, first)
         squares(1, second)
         difference(1, first)

@@ -19,8 +19,14 @@ ACT = mybir.ActivationFunctionType
 
 P = 128
 PACK = 4
+QUADRANT = 32
+PER_COLUMN = 16
+LINE = 4
 HALF = 256
-HC = HALF // 16
+LAST = PACK - 1
+MIDDLE = (1, 2)
+COPIED_ON_VECTOR = 2
+TAIL = P
 
 
 def tile_picked_ytrajcl_lse_p_kernel(
@@ -31,23 +37,38 @@ def tile_picked_ytrajcl_lse_p_kernel(
         sb = ctx.enter_context(tc.tile_pool(name="sb", bufs=1))
         ps = ctx.enter_context(tc.psum_pool(name="ps", bufs=1))
 
-        def tl(name, shape, dtype):
-            return sb.tile(shape, dtype, name=name, align_bytes=64)
+        def new_tile(name, shape, dtype, after=None):
+            return sb.tile(shape, dtype, name=name, tag=after or name, align_bytes=64)
 
-        offs_t = tl("offs_t", [P, S // 16], U16)
-        nxt_t = tl("nxt_t", [P, S // 16], U16)
-        road_t = tl("road_t", [P, Z // 16], U16)
-        con_t = tl("con_t", [P, Z // 16], U16)
-        xs = sb.tile([P, T], U8, name="xs", tag="fourth", align_bytes=64)
-        es = sb.tile([P, W], U8, name="es", tag="fifth", align_bytes=64)
-        u = tl("u", [P, PACK], F32)
-        w_raw = sb.tile([P, PACK, H], F32, name="w_raw", tag="first", align_bytes=64)
-        xw = sb.tile([P, T], I32, name="xw", tag="second", align_bytes=64)
+        def tiles(name, n, shape, dtype):
+            return [new_tile("%s%d" % (name, i), shape, dtype) for i in range(n)]
 
+        def entries(lst, cols):
+            return lst[:, cols.start // PER_COLUMN : cols.stop // PER_COLUMN]
+
+        halves = [slice(0, HALF), slice(HALF, S)]
+        first, second = halves
+        whole = slice(0, S)
+
+        offs_t = new_tile("offs_t", [P, S // PER_COLUMN], U16)
+        nxt_t = new_tile("nxt_t", [P, S // PER_COLUMN], U16)
+        road_t = new_tile("road_t", [P, Z // PER_COLUMN], U16)
+        con_t = new_tile("con_t", [P, Z // PER_COLUMN], U16)
+        xs = new_tile("xs", [P, T], U8)
+        es = new_tile("es", [P, W], U8)
+        u = new_tile("u", [P, PACK], F32)
+        w_raw = new_tile("w_raw", [P, PACK, H], F32)
+        xw = new_tile("xw", [P, T], I32)
+
+        nc.vector.memset(xs[:].bitcast(I32), 0)
         nc.vector.memset(es[:].bitcast(I32), 0)
 
-        def load_scales(queue, dst, src, q):
-            queue.dma_start(out=dst[32 * q : 32 * q + 4, :].bitcast(I32), in_=src[0, 4 * q : 4 * q + 4, :].bitcast(I32))
+        def load_scales(dst, src):
+            for q in range(P // QUADRANT):
+                nc.sync.dma_start(
+                    out=dst[QUADRANT * q : QUADRANT * q + PACK, :].bitcast(I32),
+                    in_=src[0, PACK * q : PACK * q + PACK, :].bitcast(I32),
+                )
 
         def words(src):
             return src[0].rearrange("p n t -> p (n t)").bitcast(I32)
@@ -55,112 +76,105 @@ def tile_picked_ytrajcl_lse_p_kernel(
         nc.sync.dma_start(out=u[:], in_=unit.rearrange("(p t) o -> p (t o)", t=PACK))
         nc.sync.dma_start(out=w_raw[:], in_=w1.rearrange("(p j) c -> p j c", j=PACK))
         nc.sync.dma_start(offs_t[:], offs)
-        for q in range(4):
-            rows = x_scales[0, 4 * q : 4 * q + 4, :].bitcast(I32)
-            nc.sync.dma_start(out=xs[32 * q : 32 * q + 32, :].bitcast(I32), in_=rows.unsqueeze(0).to_broadcast([8, 4, T // 4]))
-        nc.sync.dma_start(out=xw[:], in_=words(x_words))
         nc.sync.dma_start(road_t[:], road)
+        load_scales(xs, x_scales)
+        nc.sync.dma_start(out=xw[:], in_=words(x_words))
         nc.sync.dma_start(nxt_t[:], nxt)
         nc.sync.dma_start(con_t[:], con)
-        for q in range(4):
-            load_scales(nc.sync, es, e_scales, q)
+        load_scales(es, e_scales)
 
-        xg_w = tl("xg_w", [P, S], U32)
+        xg_w = new_tile("xg_w", [P, S], U32)
 
-        u_safe = tl("u_safe", [P, PACK], F32)
-        u_isq = tl("u_isq", [P, PACK], F32)
-        u_inv = tl("u_inv", [P, PACK], F32)
+        u_safe = new_tile("u_safe", [P, PACK], F32)
+        u_isq = new_tile("u_isq", [P, PACK], F32)
+        u_inv = new_tile("u_inv", [P, PACK], F32)
         nc.vector.scalar_tensor_tensor(u_safe[:], u[:], 0.0, u[:], ALU.is_equal, ALU.add)
         nc.scalar.activation(u_isq[:], u_safe[:], ACT.Abs_reciprocal_sqrt)
         nc.scalar.activation(u_inv[:], u_isq[:], ACT.Square)
 
         w_src = w_raw[:].rearrange("p j (m t) -> p t m j", t=PACK)
-        w_bf0 = tl("w_bf0", [P, P, PACK], BF16)
-        w_bf = sb.tile([P, PACK - 1, P, PACK], BF16, name="w_bf", tag="third", align_bytes=64)
-        wq_w0 = tl("wq_w0", [P, P], U32)
-        wq_s = tl("wq_s", [P, H], U8)
-        xg_s = tl("xg_s", [P, S], U8)
+        w_bf0 = new_tile("w_bf0", [P, P, PACK], BF16)
+        w_bf = new_tile("w_bf", [P, LAST, P, PACK], BF16)
+        wq_w0 = new_tile("wq_w0", [P, P], U32)
+        wq_s = new_tile("wq_s", [P, H], U8)
+        xg_s = new_tile("xg_s", [P, S], U8)
 
         nc.vector.tensor_copy(w_bf0[:], w_src[:, 0])
-        nc.scalar.copy(w_bf[:, 0], w_src[:, 1])
+        nc.scalar.copy(w_bf[:], w_src[:, 1:])
         nc.vector.tensor_copy(xg_s[:], xs[:].indirect(offs_t[:]))
-        len_t = sb.tile([P, W], F32, name="len_t", tag="fourth", align_bytes=64)
+        len_t = new_tile("len_t", [P, W], F32, after="xs")
         nc.sync.dma_start(out=len_t[:], in_=len_)
-        nc.vector.quantize_mx(out=wq_w0[:].bitcast(FP8X4), scales=wq_s[:, :P], in_=w_bf0[:].rearrange("p m j -> p (m j)"))
-        nc.vector.tensor_copy(w_bf[:, 1], w_src[:, 2])
-        nc.scalar.copy(w_bf[:, 2], w_src[:, 3])
-        ew = sb.tile([P, W], I32, name="ew", tag="first", align_bytes=64)
+        nc.vector.quantize_mx(
+            out=wq_w0[:].bitcast(FP8X4), scales=wq_s[:, :P], in_=w_bf0[:].rearrange("p m j -> p (m j)")
+        )
+        ew = new_tile("ew", [P, W], I32, after="w_raw")
         nc.sync.dma_start(out=ew[:], in_=words(e_words))
-        for c in range(2):
-            nc.vector.tensor_copy(xg_w[:, c * HALF : (c + 1) * HALF], xw[:].bitcast(U32).indirect(offs_t[:, c * HC : (c + 1) * HC]))
-        wq_w = sb.tile([P, H - P], U32, name="wq_w", tag="second", align_bytes=64)
-        nc.vector.quantize_mx(out=wq_w[:].bitcast(FP8X4), scales=wq_s[:, P:], in_=w_bf[:].rearrange("p t m j -> p (t m j)"))
-        eg_s = sb.tile([P, Z], U8, name="eg_s", tag="third", align_bytes=64)
+        for cols in halves:
+            nc.vector.tensor_copy(xg_w[:, cols], xw[:].bitcast(U32).indirect(entries(offs_t, cols)))
+        wq_w = new_tile("wq_w", [P, H - P], U32, after="xw")
+        nc.vector.quantize_mx(
+            out=wq_w[:].bitcast(FP8X4), scales=wq_s[:, P:], in_=w_bf[:].rearrange("p t m j -> p (t m j)")
+        )
+        eg_s = new_tile("eg_s", [P, Z], U8, after="w_bf")
         nc.vector.tensor_copy(eg_s[:], es[:].indirect(road_t[:]))
 
-        def tiles(name, n, shape, dtype):
-            return [tl("%s%d" % (name, i), shape, dtype) for i in range(n)]
-
         y_ps = [ps.tile([P, S], F32, name="y_ps%d" % t) for t in range(PACK)]
-        win = [tl("win%d" % t, [P, 2 * S if t in (1, 2) else S], F32) for t in range(PACK)]
+        win = [new_tile("win%d" % t, [P, 2 * S if t in MIDDLE else S], F32) for t in range(PACK)]
         uy = [win[t][:, :S] for t in range(PACK)]
-        mag = [win[t][:, S:] if t in (1, 2) else tl("mag%d" % t, [P, S], F32)[:] for t in range(PACK)]
-        own_early = sb.tile([P, 2, S], F32, name="own_early", tag="fifth", align_bytes=64)
-        own = [own_early[:, t, :] if t < 2 else tl("own%d" % t, [P, S], F32)[:] for t in range(PACK)]
+        mag = [win[t][:, S:] if t in MIDDLE else new_tile("mag%d" % t, [P, S], F32)[:] for t in range(PACK)]
+        own_early = new_tile("own_early", [P, COPIED_ON_VECTOR, S], F32, after="es")
+        own = [
+            own_early[:, t, :] if t < COPIED_ON_VECTOR else new_tile("own%d" % t, [P, S], F32)[:] for t in range(PACK)
+        ]
         vel = tiles("vel", PACK, [P, S], F32)
-        vy = [sb.tile([P, S], F32, name="vy%d" % t, tag="vy%d" % t, align_bytes=64) for t in range(PACK)]
+        vy = tiles("vy", PACK, [P, S], F32)
         y_first = ps.tile([P, HALF], F32, name="y_first", tag="reused")
-        traj = tl("traj", [P, PACK, V], F32)
+        traj = new_tile("traj", [P, PACK, V], F32)
         den = tiles("den", PACK, [P, V], F32)
-        den2 = [sb.tile([P, V], F32, name="den2_%d" % t, tag="den2_%d" % t, align_bytes=64) for t in range(PACK)]
-        rec = tl("rec", [P, PACK, V], F32)
+        den2 = tiles("den2_", PACK, [P, V], F32)
+        rec = new_tile("rec", [P, PACK, V], F32)
         hid = tiles("hid", 2, [P, P, PACK], BF16)
         hq_w = tiles("hq_w", 2, [P, P], U32)
         hq_s = tiles("hq_s", 2, [P, P], U8)
-        dwin = [sb.tile([P, 2 * Z], F32, name="dwin%d" % h, tag="dwin%d" % h, align_bytes=64) for h in range(2)]
+        dwin = tiles("dwin", 2, [P, 2 * Z], F32)
         ds = [dwin[h][:, Z:] for h in range(2)]
         sq = tiles("sq", 2, [P, Z], F32)
         sq7 = [dwin[h][:, :Z] for h in range(2)]
         dif = tiles("dif", 2, [P, Z], F32)
         gap = tiles("gap", 2, [P, Z], F32)
-        ex = tl("ex", [P, 2, Z], F32)
+        ex = new_tile("ex", [P, 2, Z], F32)
         res = tiles("res", 2, [P, Z], F32)
 
-        halves = [slice(0, HALF), slice(HALF, S)]
-        whole = slice(0, S)
-
         def product(t, dst, cols):
-            rows = slice(t * P, (t + 1) * P)
             codes = wq_w0[:] if t == 0 else wq_w[:, (t - 1) * P : t * P]
             nc.tensor.matmul_mx(
-                out=dst, lhsT=codes.bitcast(FP8X4), lhsT_scale=wq_s[:, rows],
+                out=dst, lhsT=codes.bitcast(FP8X4), lhsT_scale=wq_s[:, t * P : (t + 1) * P],
                 rhs=xg_w[:, cols].bitcast(FP8X4), rhs_scale=xg_s[:, cols], start=True, stop=True,
             )
 
         def scaled(t, dst, src):
             nc.scalar.activation(dst, src, ACT.Copy, scale=u[:, t : t + 1])
 
-        product(0, y_first[:], halves[0])
-        product(0, y_ps[0][:, halves[1]], halves[1])
-        scaled(0, uy[0][:, halves[0]], y_first[:])
-        scaled(0, uy[0][:, halves[1]], y_ps[0][:, halves[1]])
-        nc.scalar.activation(mag[0][:, halves[0]], y_first[:], ACT.Abs)
-        nc.scalar.activation(mag[0][:, halves[1]], y_ps[0][:, halves[1]], ACT.Abs)
+        product(0, y_first[:], first)
+        product(0, y_ps[0][:, second], second)
+        scaled(0, uy[0][:, first], y_first[:])
+        scaled(0, uy[0][:, second], y_ps[0][:, second])
+        nc.scalar.activation(mag[0][:, first], y_first[:], ACT.Abs)
+        nc.scalar.activation(mag[0][:, second], y_ps[0][:, second], ACT.Abs)
         for t in range(1, PACK):
             product(t, y_ps[t][:], whole)
             scaled(t, uy[t], y_ps[t][:])
-            if t > 1:
+            if t >= COPIED_ON_VECTOR:
                 nc.sync.dma_start(out=own[t], in_=uy[t])
             nc.scalar.activation(mag[t], y_ps[t][:], ACT.Abs)
 
         def copy_own(t, cols):
             nc.vector.tensor_copy(own[t][:, cols], uy[t][:, cols])
 
-        def entries(lst, cols):
-            return lst[:, cols.start // 16 : cols.stop // 16]
-
         def step(t, cols):
-            nc.vector.tensor_tensor(vel[t][:, cols], win[t][:].indirect(entries(nxt_t, cols)), own[t][:, cols], ALU.subtract)
+            nc.vector.tensor_tensor(
+                vel[t][:, cols], win[t][:].indirect(entries(nxt_t, cols)), own[t][:, cols], ALU.subtract
+            )
 
         def weigh(t, cols):
             nc.vector.tensor_tensor(vy[t][:, cols], vel[t][:, cols], mag[t][:, cols], ALU.mult)
@@ -176,17 +190,20 @@ def tile_picked_ytrajcl_lse_p_kernel(
         def hidden(h):
             cols = slice(h * P, (h + 1) * P)
             nc.vector.tensor_tensor(
-                hid[h][:].rearrange("p (c i) t -> p c t i", i=4),
-                traj[:, :, cols].rearrange("p t (c i) -> p c t i", i=4),
-                rec[:, :, cols].rearrange("p t (c i) -> p c t i", i=4),
+                hid[h][:].rearrange("p (c i) t -> p c t i", i=LINE),
+                traj[:, :, cols].rearrange("p t (c i) -> p c t i", i=LINE),
+                rec[:, :, cols].rearrange("p t (c i) -> p c t i", i=LINE),
                 ALU.mult,
             )
 
         def quantise_hidden(h):
-            nc.vector.quantize_mx(out=hq_w[h][:].bitcast(FP8X4), scales=hq_s[h][:], in_=hid[h][:].rearrange("p v t -> p (v t)"))
+            nc.vector.quantize_mx(
+                out=hq_w[h][:].bitcast(FP8X4), scales=hq_s[h][:], in_=hid[h][:].rearrange("p v t -> p (v t)")
+            )
 
         def scores(h, c):
-            bank = ps.tile([P, HALF], F32, name="sc%d%d" % (h, c), tag="reused" if (h, c) == (1, 1) else "sc%d%d" % (h, c))
+            name = "sc%d%d" % (h, c)
+            bank = ps.tile([P, HALF], F32, name=name, tag="reused" if (h, c) == (1, 1) else name)
             nc.tensor.matmul_mx(
                 out=bank[:], lhsT=hq_w[h][:].bitcast(FP8X4), lhsT_scale=hq_s[h][:],
                 rhs=eg_w[:, halves[c]].bitcast(FP8X4), rhs_scale=eg_s[:, halves[c]], start=True, stop=True,
@@ -204,7 +221,9 @@ def tile_picked_ytrajcl_lse_p_kernel(
             nc.scalar.activation(sq[h][:, cols], ds[h][:, cols], ACT.Square)
 
         def difference(h, cols):
-            nc.vector.tensor_tensor(dif[h][:, cols], dwin[h][:].indirect(entries(con_t, cols)), sq[h][:, cols], ALU.subtract)
+            nc.vector.tensor_tensor(
+                dif[h][:, cols], dwin[h][:].indirect(entries(con_t, cols)), sq[h][:, cols], ALU.subtract
+            )
 
         def gaps(h, cols):
             nc.scalar.activation(gap[h][:, cols], dif[h][:, cols], ACT.Abs)
@@ -221,40 +240,38 @@ def tile_picked_ytrajcl_lse_p_kernel(
             nc.vector.tensor_tensor(res[h][:, cols], lg[:, cols], low[:, h, cols], ALU.subtract)
             nc.sync.dma_start(out=out[h * P : (h + 1) * P, cols], in_=res[h][:, cols])
 
-        last = PACK - 1
-        copy_own(0, halves[0])
-        copy_own(0, halves[1])
-        step(0, halves[0])
-        step(0, halves[1])
+        copy_own(0, first)
+        copy_own(0, second)
+        step(0, first)
+        step(0, second)
         copy_own(1, whole)
         weigh(0, whole)
-        for t in range(1, last):
+        for t in MIDDLE:
             step(t, whole)
             pair(t - 1, whole)
             weigh(t, whole)
-            if t == 1:
-                len_g = sb.tile([P, Z], F32, name="len_g", tag="den2_0", align_bytes=64)
+            if t == MIDDLE[0]:
+                len_g = new_tile("len_g", [P, Z], F32, after="den2_0")
                 nc.scalar.activation(len_g[:], len_t[:].indirect(road_t[:]), ACT.Copy)
-        step(last, halves[0])
-        pair(last - 1, whole)
-        eg_w = sb.tile([P, Z], U32, name="eg_w", tag="vy%d" % (last - 1), align_bytes=64)
+        step(LAST, first)
+        pair(LAST - 1, whole)
+        eg_w = new_tile("eg_w", [P, Z], U32, after="vy%d" % (LAST - 1))
 
-        def fetch_roads(c):
-            nc.vector.tensor_copy(eg_w[:, halves[c]], ew[:].bitcast(U32).indirect(road_t[:, c * HC : (c + 1) * HC]))
+        def fetch_roads(cols):
+            nc.vector.tensor_copy(eg_w[:, cols], ew[:].bitcast(U32).indirect(entries(road_t, cols)))
 
-        weigh(last, halves[0])
-        step(last, halves[1])
-        pair(last, halves[0])
-        weigh(last, halves[1])
-        fetch_roads(0)
-        pair(last, halves[1])
-        warm = tl("warm", [P, 1], F32)
-        nc.scalar.activation(warm[:], rec[:, last, V - 1 : V], ACT.Exp)
-        first, second = halves
+        weigh(LAST, first)
+        step(LAST, second)
+        pair(LAST, first)
+        weigh(LAST, second)
+        fetch_roads(first)
+        pair(LAST, second)
+        warm = new_tile("warm", [P, 1], F32)
+        nc.scalar.activation(warm[:], rec[:, LAST, V - 1 : V], ACT.Exp)
         hidden(0)
         quantise_hidden(0)
         bank00 = scores(0, 0)
-        fetch_roads(1)
+        fetch_roads(second)
         bank01 = scores(0, 1)
         hidden(1)
         distances(0, 0, bank00)
@@ -275,7 +292,7 @@ def tile_picked_ytrajcl_lse_p_kernel(
         squares(1, second)
         difference(1, first)
         difference(1, second)
-        low = sb.tile([P, 2, Z], F32, name="low", tag="dwin1", align_bytes=64)
+        low = new_tile("low", [P, 2, Z], F32, after="dwin1")
         gaps(0, whole)
         gaps(1, first)
         decay(0, whole)
@@ -284,6 +301,6 @@ def tile_picked_ytrajcl_lse_p_kernel(
         decay(1, second)
         smaller(0)
         smaller(1)
-        finish(0, slice(0, Z))
-        finish(1, slice(0, 3 * P))
-        finish(1, slice(3 * P, Z))
+        finish(0, whole)
+        finish(1, slice(0, Z - TAIL))
+        finish(1, slice(Z - TAIL, Z))

from contextlib import ExitStack
import math

import concourse.mybir as mybir

K, T, S, H, Z, W = 512, 2048, 512, 512, 512, 2048
V = S // 2
FLOPS = 2 * K * H * S + 2 * H * V * Z

F32 = mybir.dt.float32
BF16 = mybir.dt.bfloat16
I32 = mybir.dt.int32
U32 = mybir.dt.uint32
U16 = mybir.dt.uint16
U8 = mybir.dt.uint8
FP8X4 = mybir.dt.float8_e4m3fn_x4
ALU = mybir.AluOpType
ACT = mybir.ActivationFunctionType

P = 128
PACK = 4
QUADRANT = 32
PER_COLUMN = 16
LINE = 4
HALF = 256
LAST = PACK - 1
MIDDLE = (1, 2)
COPIED_ON_VECTOR = 2
TAIL = P


def tile_picked_ytrajcl_lse_p_kernel(
    tc, x_words, x_scales, w1, e_words, e_scales, unit, len_, offs, nxt, road, con, out
):
    nc = tc.nc
    with ExitStack() as ctx:
        sb = ctx.enter_context(tc.tile_pool(name="sb", bufs=1))
        ps = ctx.enter_context(tc.psum_pool(name="ps", bufs=1))

        def new_tile(name, shape, dtype, after=None):
            return sb.tile(shape, dtype, name=name, tag=after or name, align_bytes=64)

        def tiles(name, n, shape, dtype):
            return [new_tile("%s%d" % (name, i), shape, dtype) for i in range(n)]

        def entries(lst, cols):
            return lst[:, cols.start // PER_COLUMN : cols.stop // PER_COLUMN]

        halves = [slice(0, HALF), slice(HALF, S)]
        first, second = halves
        whole = slice(0, S)

        offs_t = new_tile("offs_t", [P, S // PER_COLUMN], U16)
        nxt_t = new_tile("nxt_t", [P, S // PER_COLUMN], U16)
        road_t = new_tile("road_t", [P, Z // PER_COLUMN], U16)
        con_t = new_tile("con_t", [P, Z // PER_COLUMN], U16)
        xs = new_tile("xs", [P, T], U8)
        es = new_tile("es", [P, W], U8)
        u = new_tile("u", [P, PACK], F32)
        w_raw = new_tile("w_raw", [P, PACK, H], F32)
        xw = new_tile("xw", [P, T], I32)

        nc.vector.memset(xs[:].bitcast(I32), 0)
        nc.vector.memset(es[:].bitcast(I32), 0)

        def load_scales(dst, src):
            for q in range(P // QUADRANT):
                nc.sync.dma_start(
                    out=dst[QUADRANT * q : QUADRANT * q + PACK, :].bitcast(I32),
                    in_=src[0, PACK * q : PACK * q + PACK, :].bitcast(I32),
                )

        def words(src):
            return src[0].rearrange("p n t -> p (n t)").bitcast(I32)

        nc.sync.dma_start(out=u[:], in_=unit.rearrange("(p t) o -> p (t o)", t=PACK))
        nc.sync.dma_start(out=w_raw[:], in_=w1.rearrange("(p j) c -> p j c", j=PACK))
        nc.sync.dma_start(offs_t[:], offs)
        nc.sync.dma_start(road_t[:], road)
        load_scales(xs, x_scales)
        nc.sync.dma_start(out=xw[:], in_=words(x_words))
        nc.sync.dma_start(nxt_t[:], nxt)
        nc.sync.dma_start(con_t[:], con)
        load_scales(es, e_scales)

        xg_w = new_tile("xg_w", [P, S], U32)

        u_safe = new_tile("u_safe", [P, PACK], F32)
        u_isq = new_tile("u_isq", [P, PACK], F32)
        u_inv = new_tile("u_inv", [P, PACK], F32)
        nc.vector.scalar_tensor_tensor(u_safe[:], u[:], 0.0, u[:], ALU.is_equal, ALU.add)
        nc.scalar.activation(u_isq[:], u_safe[:], ACT.Abs_reciprocal_sqrt)
        nc.scalar.activation(u_inv[:], u_isq[:], ACT.Square)

        w_src = w_raw[:].rearrange("p j (m t) -> p t m j", t=PACK)
        w_bf0 = new_tile("w_bf0", [P, P, PACK], BF16)
        w_bf = new_tile("w_bf", [P, LAST, P, PACK], BF16)
        wq_w0 = new_tile("wq_w0", [P, P], U32)
        wq_s = new_tile("wq_s", [P, H], U8)
        xg_s = new_tile("xg_s", [P, S], U8)

        nc.vector.tensor_copy(w_bf0[:], w_src[:, 0])
        nc.scalar.copy(w_bf[:], w_src[:, 1:])
        nc.vector.tensor_copy(xg_s[:], xs[:].indirect(offs_t[:]))
        len_t = new_tile("len_t", [P, W], F32, after="xs")
        nc.sync.dma_start(out=len_t[:], in_=len_)
        nc.vector.quantize_mx(
            out=wq_w0[:].bitcast(FP8X4), scales=wq_s[:, :P], in_=w_bf0[:].rearrange("p m j -> p (m j)")
        )
        ew = new_tile("ew", [P, W], I32, after="w_raw")
        nc.sync.dma_start(out=ew[:], in_=words(e_words))
        for cols in halves:
            nc.vector.tensor_copy(xg_w[:, cols], xw[:].bitcast(U32).indirect(entries(offs_t, cols)))
        wq_w = new_tile("wq_w", [P, H - P], U32, after="xw")
        nc.vector.quantize_mx(
            out=wq_w[:].bitcast(FP8X4), scales=wq_s[:, P:], in_=w_bf[:].rearrange("p t m j -> p (t m j)")
        )
        eg_s = new_tile("eg_s", [P, Z], U8, after="w_bf")
        nc.vector.tensor_copy(eg_s[:], es[:].indirect(road_t[:]))

        y_ps = [ps.tile([P, S], F32, name="y_ps%d" % t) for t in range(PACK)]
        win = [new_tile("win%d" % t, [P, 2 * S if t in MIDDLE else S], F32) for t in range(PACK)]
        uy = [win[t][:, :S] for t in range(PACK)]
        mag = [win[t][:, S:] if t in MIDDLE else new_tile("mag%d" % t, [P, S], F32)[:] for t in range(PACK)]
        own_early = new_tile("own_early", [P, COPIED_ON_VECTOR, S], F32, after="es")
        own = [
            own_early[:, t, :] if t < COPIED_ON_VECTOR else new_tile("own%d" % t, [P, S], F32)[:] for t in range(PACK)
        ]
        vel = tiles("vel", PACK, [P, S], F32)
        vy = tiles("vy", PACK, [P, S], F32)
        y_first = ps.tile([P, HALF], F32, name="y_first", tag="reused")
        traj = new_tile("traj", [P, PACK, V], F32)
        den = tiles("den", PACK, [P, V], F32)
        den2 = tiles("den2_", PACK, [P, V], F32)
        rec = new_tile("rec", [P, PACK, V], F32)
        hid = tiles("hid", 2, [P, P, PACK], BF16)
        hq_w = tiles("hq_w", 2, [P, P], U32)
        hq_s = tiles("hq_s", 2, [P, P], U8)
        dwin = tiles("dwin", 2, [P, 2 * Z], F32)
        ds = [dwin[h][:, Z:] for h in range(2)]
        sq = tiles("sq", 2, [P, Z], F32)
        sq7 = [dwin[h][:, :Z] for h in range(2)]
        dif = tiles("dif", 2, [P, Z], F32)
        gap = tiles("gap", 2, [P, Z], F32)
        ex = new_tile("ex", [P, 2, Z], F32)
        res = tiles("res", 2, [P, Z], F32)

        def product(t, dst, cols):
            codes = wq_w0[:] if t == 0 else wq_w[:, (t - 1) * P : t * P]
            nc.tensor.matmul_mx(
                out=dst, lhsT=codes.bitcast(FP8X4), lhsT_scale=wq_s[:, t * P : (t + 1) * P],
                rhs=xg_w[:, cols].bitcast(FP8X4), rhs_scale=xg_s[:, cols], start=True, stop=True,
            )

        def scaled(t, dst, src):
            nc.scalar.activation(dst, src, ACT.Copy, scale=u[:, t : t + 1])

        product(0, y_first[:], first)
        product(0, y_ps[0][:, second], second)
        scaled(0, uy[0][:, first], y_first[:])
        scaled(0, uy[0][:, second], y_ps[0][:, second])
        nc.scalar.activation(mag[0][:, first], y_first[:], ACT.Abs)
        nc.scalar.activation(mag[0][:, second], y_ps[0][:, second], ACT.Abs)
        for t in range(1, PACK):
            product(t, y_ps[t][:], whole)
            scaled(t, uy[t], y_ps[t][:])
            if t >= COPIED_ON_VECTOR:
                nc.sync.dma_start(out=own[t], in_=uy[t])
            nc.scalar.activation(mag[t], y_ps[t][:], ACT.Abs)

        def copy_own(t, cols):
            nc.vector.tensor_copy(own[t][:, cols], uy[t][:, cols])

        def step(t, cols):
            nc.vector.tensor_tensor(
                vel[t][:, cols], win[t][:].indirect(entries(nxt_t, cols)), own[t][:, cols], ALU.subtract
            )

        def weigh(t, cols):
            nc.vector.tensor_tensor(vy[t][:, cols], vel[t][:, cols], mag[t][:, cols], ALU.mult)

        def pair(t, cols):
            vs = slice(cols.start // 2, cols.stop // 2)
            pairs = vy[t][:, cols].rearrange("p (v d) -> p v d", d=2)
            nc.vector.tensor_tensor(traj[:, t, vs], pairs[:, :, 0], pairs[:, :, 1], ALU.add)
            nc.scalar.activation(den[t][:, vs], traj[:, t, vs], ACT.Abs, scale=u_inv[:, t : t + 1])
            nc.scalar.activation(den2[t][:, vs], den[t][:, vs], ACT.Square, bias=0.8)
            nc.scalar.activation(rec[:, t, vs], den2[t][:, vs], ACT.Abs_reciprocal_sqrt)

        def hidden(h):
            cols = slice(h * P, (h + 1) * P)
            nc.vector.tensor_tensor(
                hid[h][:].rearrange("p (c i) t -> p c t i", i=LINE),
                traj[:, :, cols].rearrange("p t (c i) -> p c t i", i=LINE),
                rec[:, :, cols].rearrange("p t (c i) -> p c t i", i=LINE),
                ALU.mult,
            )

        def quantise_hidden(h):
            nc.vector.quantize_mx(
                out=hq_w[h][:].bitcast(FP8X4), scales=hq_s[h][:], in_=hid[h][:].rearrange("p v t -> p (v t)")
            )

        def scores(h, c):
            name = "sc%d%d" % (h, c)
            bank = ps.tile([P, HALF], F32, name=name, tag="reused" if (h, c) == (1, 1) else name)
            nc.tensor.matmul_mx(
                out=bank[:], lhsT=hq_w[h][:].bitcast(FP8X4), lhsT_scale=hq_s[h][:],
                rhs=eg_w[:, halves[c]].bitcast(FP8X4), rhs_scale=eg_s[:, halves[c]], start=True, stop=True,
            )
            return bank

        def distances(h, c, bank):
            cols = halves[c]
            nc.vector.tensor_tensor(ds[h][:, cols], bank[:], len_g[:, cols], ALU.subtract)

        def window_squares(h, cols):
            nc.scalar.activation(sq7[h][:, cols], ds[h][:, cols], ACT.Square, scale=math.sqrt(0.7))

        def squares(h, cols):
            nc.scalar.activation(sq[h][:, cols], ds[h][:, cols], ACT.Square)

        def difference(h, cols):
            nc.vector.tensor_tensor(
                dif[h][:, cols], dwin[h][:].indirect(entries(con_t, cols)), sq[h][:, cols], ALU.subtract
            )

        def gaps(h, cols):
            nc.scalar.activation(gap[h][:, cols], dif[h][:, cols], ACT.Abs)

        def decay(h, cols):
            nc.scalar.activation(ex[:, h, cols], gap[h][:, cols], ACT.Exp, scale=-1.0)

        def smaller(h):
            nc.vector.scalar_tensor_tensor(low[:, h, :], dif[h][:], 0.0, sq[h][:], ALU.min, ALU.add)

        def finish(h, cols):
            lg = gap[1] if h == 0 else ex[:, 0, :]
            nc.scalar.activation(lg[:, cols], ex[:, h, cols], ACT.Ln, bias=1.0)
            nc.vector.tensor_tensor(res[h][:, cols], lg[:, cols], low[:, h, cols], ALU.subtract)
            nc.sync.dma_start(out=out[h * P : (h + 1) * P, cols], in_=res[h][:, cols])

        copy_own(0, first)
        copy_own(0, second)
        step(0, first)
        step(0, second)
        copy_own(1, whole)
        weigh(0, whole)
        for t in MIDDLE:
            step(t, whole)
            pair(t - 1, whole)
            weigh(t, whole)
            if t == MIDDLE[0]:
                len_g = new_tile("len_g", [P, Z], F32, after="den2_0")
                nc.scalar.activation(len_g[:], len_t[:].indirect(road_t[:]), ACT.Copy)
        step(LAST, first)
        pair(LAST - 1, whole)
        eg_w = new_tile("eg_w", [P, Z], U32, after="vy%d" % (LAST - 1))

        def fetch_roads(cols):
            nc.vector.tensor_copy(eg_w[:, cols], ew[:].bitcast(U32).indirect(entries(road_t, cols)))

        weigh(LAST, first)
        step(LAST, second)
        pair(LAST, first)
        weigh(LAST, second)
        fetch_roads(first)
        pair(LAST, second)
        warm = new_tile("warm", [P, 1], F32)
        nc.scalar.activation(warm[:], rec[:, LAST, V - 1 : V], ACT.Exp)
        hidden(0)
        quantise_hidden(0)
        bank00 = scores(0, 0)
        fetch_roads(second)
        bank01 = scores(0, 1)
        hidden(1)
        distances(0, 0, bank00)
        quantise_hidden(1)
        bank10 = scores(1, 0)
        bank11 = scores(1, 1)
        distances(0, 1, bank01)
        window_squares(0, first)
        window_squares(0, second)
        nc.vector.tensor_tensor(sq[0][:, first], ds[0][:, first], ds[0][:, first], ALU.mult)
        squares(0, second)
        distances(1, 0, bank10)
        distances(1, 1, bank11)
        difference(0, whole)
        window_squares(1, first)
        window_squares(1, second)
        squares(1, first)
        squares(1, second)
        difference(1, first)
        difference(1, second)
        low = new_tile("low", [P, 2, Z], F32, after="dwin1")
        gaps(0, whole)
        gaps(1, first)
        decay(0, whole)
        nc.vector.scalar_tensor_tensor(gap[1][:, second], dif[1][:, second], -1.0, dif[1][:, second], ALU.mult, ALU.max)
        decay(1, first)
        decay(1, second)
        smaller(0)
        smaller(1)
        finish(0, whole)
        finish(1, slice(0, Z - TAIL))
        finish(1, slice(Z - TAIL, Z))
